import numpy as np
import ml_dtypes


def mxq(x, axis, fmt="e4m3"):
    dtype, down = {"e4m3": (ml_dtypes.float8_e4m3fn, 7), "e5m2": (ml_dtypes.float8_e5m2, 14)}[fmt]
    v = np.moveaxis(np.asarray(x, np.float32).astype(ml_dtypes.bfloat16).astype(np.float64), axis, -1)
    blocks = v.reshape(v.shape[:-1] + (-1, 32))
    amax = np.abs(blocks).max(-1, keepdims=True)
    byte = np.maximum(np.where(amax > 0, np.frexp(amax)[1] - 1 + 127, 0) - down, 1)
    scale = np.exp2(byte - 127.0)
    codes = (blocks / scale).astype(np.float32).astype(dtype).astype(np.float64)
    return np.moveaxis((codes * scale).reshape(v.shape), -1, axis)


WIDE = False


def mx_kscale(k):
    if not WIDE:
        return np.ones(k)
    levels = np.array([10, -10, 5, -5, 0])
    if k % 512:
        return np.exp2(np.random.permutation(np.resize(levels, k // 32))).repeat(32)
    a = np.empty((k // 512, 16))
    for p in range(k // 512):
        a[p, :8] = np.random.permutation(np.resize(levels, 8))
        for g in range(8):
            far = levels[np.abs(levels - a[p, g]) >= 10]
            a[p, g + 8] = far[np.random.randint(len(far))]
    return np.exp2(a.ravel()).repeat(32)


BF16 = ml_dtypes.bfloat16


def bf(x):
    return np.asarray(x, np.float32).astype(BF16)


def f64(x):
    return np.asarray(x).astype(np.float64)


E2M1 = np.array([0.0, 0.5, 1.0, 1.5, 2.0, 3.0, 4.0, 6.0, -0.0, -0.5, -1.0, -1.5, -2.0, -3.0, -4.0, -6.0])


def pack_weight(w, fmt):
    k, n = w.shape
    w = f64(bf(w)).reshape(k // 32, 32, n)
    amax = np.abs(w).max(1)
    if fmt == "e4m3":
        byte = np.frexp(amax)[1] - 1 + 127 - 7
    else:
        mant, ex = np.frexp(amax / 6.0)
        byte = np.where(mant > 0.5, ex, ex - 1) + 127
    byte = np.clip(np.where(amax > 0, byte, 1), 1, 254)
    scaled = (w * np.exp2(127.0 - byte)[:, None, :]).reshape(k, n).astype(np.float32)
    by_word = np.ascontiguousarray(scaled.reshape(k // 512, 128, 4, n).transpose(0, 1, 3, 2))
    if fmt == "e4m3":
        words = by_word.astype(ml_dtypes.float8_e4m3fn).view(np.uint8)
    else:
        c = by_word.astype(ml_dtypes.float4_e2m1fn).view(np.uint8) & 0xF
        words = c[..., 0::2] | (c[..., 1::2] << 4)
    return np.ascontiguousarray(words), np.ascontiguousarray(byte.astype(np.uint8).reshape(k // 512, 16, n))


def unpack_weight(words, scales, fmt):
    g, p, n, _ = words.shape
    if fmt == "e4m3":
        vals = np.ascontiguousarray(words).view(ml_dtypes.float8_e4m3fn).astype(np.float64)
    else:
        nib = np.empty((g, p, n, 4), np.uint8)
        nib[..., 0::2] = words & 0xF
        nib[..., 1::2] = words >> 4
        vals = E2M1[nib]
    vals = vals * np.repeat(np.exp2(scales.astype(np.float64) - 127.0), 8, axis=1)[..., None]
    return vals.transpose(0, 1, 3, 2).reshape(g * 512, n)
def pack4(w):
    words, scales = pack_weight(w, "e2m1")
    return words.reshape(words.shape[0], 128, -1), scales


def unpack4(words, scales):
    return unpack_weight(words.reshape(words.shape[0], 128, -1, 2), scales, "e2m1")


K, T, F, C = 1024, 2048, 1024, 512


def setup_inputs():
    s = mx_kscale(K)
    t = mx_kscale(F)
    x_words, x_scales = pack4(np.random.standard_normal((K, T)) * s[:, None])
    bank_words, bank_scales = pack4(np.random.standard_normal((K, F)) / np.sqrt(K) / s[:, None])
    mix_words, mix_scales = pack_weight(np.random.standard_normal((F, C)) / np.sqrt(F) / t[:, None], "e4m3")
    return {"x_words": x_words, "x_scales": x_scales,
            "bank_words": bank_words, "bank_scales": bank_scales,
            "gain": bf((1 + 0.1 * np.random.standard_normal(F)) * t),
            "mix_words": mix_words, "mix_scales": mix_scales,
            "bias": bf(0.3 * np.random.standard_normal(C))}


def reference(x_words, x_scales, bank_words, bank_scales, gain, mix_words, mix_scales, bias):
    x = unpack4(x_words, x_scales)
    bank = unpack4(bank_words, bank_scales)
    mix = unpack_weight(mix_words, mix_scales, "e4m3")
    y = bank.T @ x
    h = np.abs(y) * f64(gain)[:, None]
    z = mix.T @ mxq(h, 0, "e4m3")
    return z + f64(bias)[:, None]

@@ -1,0 +1,256 @@
+from contextlib import ExitStack
+
+import concourse.mybir as mybir
+
+SAMPLES, FRAMES, FILTERS, CHANNELS = 1024, 2048, 1024, 512
+FLOPS = 2 * SAMPLES * FRAMES * FILTERS + 2 * FILTERS * FRAMES * CHANNELS
+
+F32 = mybir.dt.float32
+BF16 = mybir.dt.bfloat16
+I32 = mybir.dt.int32
+U32 = mybir.dt.uint32
+U8 = mybir.dt.uint8
+FP8X4 = mybir.dt.float8_e4m3fn_x4
+FP4X4 = mybir.dt.float4_e2m1fn_x4
+ALU = mybir.AluOpType
+ACT = mybir.ActivationFunctionType
+
+P = 128
+PACK = 4
+K_PASS = P * PACK
+PASSES = 2
+X_TILE = 512
+CHUNKS = [(0, 512), (512, 512), (1024, 512), (1536, 256), (1792, 256)]
+F_TILES = FILTERS // P
+C_TILES = CHANNELS // P
+LAG = 5
+
+
+def tile_filter_bank_channel_mixer_s4_kernel(
+    tc, x_words, x_scales, bank_words, bank_scales, gain, mix_words, mix_scales, bias, out
+):
+    nc = tc.nc
+    with ExitStack() as ctx:
+        keep = ctx.enter_context(tc.tile_pool(name="keep", bufs=1))
+        work = ctx.enter_context(tc.tile_pool(name="work", bufs=3))
+        psum = ctx.enter_context(tc.psum_pool(name="psum", bufs=4))
+        ctx.enter_context(nc.allow_non_contiguous_dma(reason="small gain and bias columns"))
+        ctx.enter_context(tc.manual_schedule())
+
+        x_sb = []
+        for j in range(FRAMES // X_TILE):
+            xt = keep.tile([P, PASSES, 2 * X_TILE], U8, name="x%d" % j, align_bytes=64)
+            x_sb.append(xt)
+        b_raw = []
+        for h in range(2):
+            bt = keep.tile([P, PASSES, 2 * K_PASS], U8, name="braw%d" % h, align_bytes=64)
+            b_raw.append(bt)
+        b_sb, bs_sb = [], []
+        for f in range(F_TILES):
+            bt = keep.tile([P, PASSES, 2 * P], U8, name="b%d" % f, align_bytes=64)
+            b_sb.append(bt)
+            st = keep.tile([P, PASSES, P], U8, name="bs%d" % f, align_bytes=64)
+            bs_sb.append(st)
+        m_sb = keep.tile([P, PASSES, 4 * CHANNELS], U8, name="mixw", align_bytes=64)
+        bs_raw = keep.tile([P, PASSES * FILTERS], U8, name="bsraw", align_bytes=64)
+        xs_first = keep.tile([P, PASSES * X_TILE], U8, name="xsfirst", align_bytes=64)
+        xs_rest = keep.tile([P, PASSES * (FRAMES - X_TILE)], U8, name="xsrest", align_bytes=64)
+        ms = keep.tile([P, PASSES * CHANNELS], U8, name="ms", align_bytes=64)
+        gain_bf = keep.tile([P, F_TILES], BF16, name="gainbf")
+        gain_f = keep.tile([P, F_TILES], F32, name="gainf")
+        sgn = keep.tile([P, F_TILES], F32, name="sgn")
+        bias_bf = keep.tile([P, C_TILES, 2], BF16, name="biasbf")
+        bias_f = keep.tile([P, C_TILES], F32, name="biasf")
+        dummy = keep.tile([P, 1], F32, name="dummy")
+
+        def load_bank(h):
+            nc.sync.dma_start(
+                out=b_raw[h][:],
+                in_=bank_words[:, :, 2 * K_PASS * h : 2 * K_PASS * (h + 1)].rearrange("g p b -> p g b"),
+            )
+
+        def load_x(j):
+            nc.sync.dma_start(
+                out=x_sb[j][:],
+                in_=x_words[:, :, 2 * X_TILE * j : 2 * X_TILE * (j + 1)].rearrange("g p b -> p g b"),
+            )
+
+        def load_scales(tile, src, r):
+            nc.sync.dma_start(
+                out=tile[r:P:32, :].rearrange("p (g n) -> p g n", g=PASSES).bitcast(I32),
+                in_=src.rearrange("g (q r) n -> r q g n", r=4)[r].bitcast(I32),
+            )
+
+        nc.vector.memset(bs_raw[:].bitcast(I32), 0)
+        nc.vector.memset(xs_first[:].bitcast(I32), 0)
+        nc.vector.memset(xs_rest[:].bitcast(I32), 0)
+        nc.vector.memset(ms[:].bitcast(I32), 0)
+        nc.vector.memset(dummy[:], 0.0)
+        nc.scalar.activation(out=dummy[:], in_=dummy[:], func=ACT.Abs)
+
+        load_bank(0)
+        nc.gpsimd.dma_start(
+            out=x_sb[0][:].bitcast(I32),
+            in_=x_words[:, :, 0 : 2 * X_TILE].rearrange("g p b -> p g b").bitcast(I32),
+        )
+        nc.gpsimd.dma_start(
+            out=gain_bf[:].rearrange("p (h t) -> p h t", t=PACK), in_=gain.rearrange("(h p t) -> p h t", p=P, t=PACK)
+        )
+        for r in range(4):
+            load_scales(bs_raw, bank_scales, r)
+        for r in range(4):
+            load_scales(xs_first, x_scales[:, :, 0:X_TILE], r)
+        load_bank(1)
+        for r in range(4):
+            load_scales(xs_rest, x_scales[:, :, X_TILE:FRAMES], r)
+        load_x(1)
+        for r in range(4):
+            load_scales(ms, mix_scales, r)
+        nc.sync.dma_start(out=m_sb[:], in_=mix_words.rearrange("g p n t -> p g (n t)"))
+        nc.gpsimd.dma_start(
+            out=bias_bf[:, :, 0:1], in_=bias.rearrange("(c p o) -> p c o", p=P, o=1)
+        )
+        load_x(2)
+        load_x(3)
+
+        def permute(f):
+            h, t = divmod(f, PACK)
+            nc.vector.tensor_copy(
+                out=b_sb[f][:].rearrange("p g (m b) -> p g m b", b=2),
+                in_=b_raw[h][:].rearrange("p g (m t b) -> p t g m b", t=PACK, b=2)[:, t],
+            )
+            nc.vector.tensor_copy(
+                out=bs_sb[f][:],
+                in_=bs_raw[:].rearrange("p (g h m t) -> p h t g m", g=PASSES, h=2, t=PACK)[:, h, t],
+            )
+
+        sub = {}
+        ymap = {}
+        grouped = {}
+        codes = {}
+        zmap = {}
+
+        def x_scale_columns(g, n0, w):
+            if n0 < X_TILE:
+                return xs_first[:, g * X_TILE + n0 : g * X_TILE + n0 + w]
+            start = g * (FRAMES - X_TILE) + n0 - X_TILE
+            return xs_rest[:, start : start + w]
+
+        def bank_pass(k):
+            i, f = divmod(k, F_TILES)
+            n0, w = CHUNKS[i]
+            j, o = divmod(n0, X_TILE)
+            y = psum.tile([P, w], F32, name="y", tag="y", bufs=4)
+            for g in range(PASSES):
+                nc.tensor.matmul_mx(
+                    out=y[:],
+                    lhsT=b_sb[f][:, g, :].bitcast(FP4X4),
+                    lhsT_scale=bs_sb[f][:, g, :],
+                    rhs=x_sb[j][:, g, 2 * o : 2 * (o + w)].bitcast(FP4X4),
+                    rhs_scale=x_scale_columns(g, n0, w),
+                    start=(g == 0),
+                    stop=(g == PASSES - 1),
+                )
+            ymap[k] = y
+
+        def rectify(k):
+            i, f = divmod(k, F_TILES)
+            h, t = divmod(f, PACK)
+            w = CHUNKS[i][1]
+            if t == 0:
+                s = work.tile([P, PACK, w], BF16, name="s", tag="s", bufs=3, align_bytes=64)
+                sub[(i, h)] = s
+            nc.scalar.activation(
+                out=sub[(i, h)][:, t, :], in_=ymap[k][:], func=ACT.Abs, scale=gain_f[:, f : f + 1]
+            )
+
+        def sign(k):
+            i, f = divmod(k, F_TILES)
+            h, t = divmod(f, PACK)
+            nc.vector.tensor_scalar(
+                out=sub[(i, h)][:, t, :], in0=sub[(i, h)][:, t, :], scalar1=sgn[:, f : f + 1], scalar2=None, op0=ALU.mult
+            )
+
+        def interleave(i, h):
+            w = CHUNKS[i][1]
+            gr = work.tile([P, w, PACK], BF16, name="gr", tag="gr", bufs=3, align_bytes=64)
+            nc.vector.tensor_copy(out=gr[:], in_=sub[(i, h)][:].rearrange("p t n -> p n t"))
+            grouped[(i, h)] = gr
+
+        def quantize(i, h):
+            w = CHUNKS[i][1]
+            c = work.tile([P, w], U32, name="hc", tag="hc", bufs=4, align_bytes=64)
+            sc = work.tile([P, w], U8, name="hs", tag="hs", bufs=4, align_bytes=64)
+            nc.vector.quantize_mx(
+                out=c[:].bitcast(FP8X4), scales=sc[:], in_=grouped[(i, h)][:].rearrange("p n t -> p (n t)")
+            )
+            codes[(i, h)] = (c, sc)
+
+        def mix_pass(i, c, g):
+            w = CHUNKS[i][1]
+            if g == 0:
+                z = psum.tile([P, w], F32, name="z", tag="z", bufs=4)
+                zmap[(i, c)] = z
+            hc, hs = codes[(i, g)]
+            nc.tensor.matmul_mx(
+                out=zmap[(i, c)][:],
+                lhsT=m_sb[:, g, 4 * P * c : 4 * P * (c + 1)].bitcast(FP8X4),
+                lhsT_scale=ms[:, g * CHANNELS + P * c : g * CHANNELS + P * (c + 1)],
+                rhs=hc[:].bitcast(FP8X4),
+                rhs_scale=hs[:],
+                start=(g == 0),
+                stop=(g == PASSES - 1),
+            )
+
+        def finish(i, c, on_vector):
+            n0, w = CHUNKS[i]
+            o = work.tile([P, w], F32, name="o", tag="o", bufs=6, align_bytes=64)
+            z = zmap[(i, c)]
+            if on_vector:
+                nc.vector.tensor_scalar(
+                    out=o[:], in0=z[:], scalar1=bias_f[:, c : c + 1], scalar2=None, op0=ALU.add
+                )
+            else:
+                nc.scalar.activation(out=o[:], in_=z[:], func=ACT.Identity, bias=bias_f[:, c : c + 1])
+            nc.sync.dma_start(out=out[P * c : P * (c + 1), n0 : n0 + w], in_=o[:])
+
+        for f in range(PACK):
+            permute(f)
+        nc.vector.tensor_copy(out=gain_f[:], in_=gain_bf[:])
+        nc.vector.tensor_scalar(out=sgn[:], in0=gain_f[:], scalar1=0.0, scalar2=2.0, op0=ALU.is_ge, op1=ALU.mult)
+        nc.vector.tensor_scalar(out=sgn[:], in0=sgn[:], scalar1=-1.0, scalar2=None, op0=ALU.add)
+
+        steps = len(CHUNKS) * F_TILES
+        for k in range(steps + 1):
+            if k < steps:
+                bank_pass(k)
+                rectify(k)
+            if k >= 1:
+                sign(k - 1)
+            if k < PACK:
+                permute(PACK + k)
+            if k == 4:
+                nc.vector.tensor_copy(out=bias_f[:], in_=bias_bf[:, :, 0])
+            d = k - (F_TILES - 1 + LAG)
+            if k < steps and d >= 0 and d % 2 == 0:
+                i, c = divmod(d // 2, C_TILES)
+                for g in range(PASSES):
+                    mix_pass(i, c, g)
+                finish(i, c, c == 1)
+            if k >= 4 and k % 4 == 0:
+                interleave((k - 1) // F_TILES, ((k - 1) // PACK) % 2)
+            if k >= 5 and k % 4 == 1:
+                quantize((k - 2) // F_TILES, ((k - 2) // PACK) % 2)
+        last = len(CHUNKS) - 1
+        quantize(last, 1)
+        first_left = (steps - 1 - (F_TILES - 1 + LAG)) // 2 + 1
+        for u in range(first_left, last * C_TILES):
+            i, c = divmod(u, C_TILES)
+            for g in range(PASSES):
+                mix_pass(i, c, g)
+            finish(i, c, c == 1)
+        for g in range(PASSES):
+            for c in range(C_TILES):
+                mix_pass(last, c, g)
+        for c in range(C_TILES):
+            finish(last, c, c % 2 == 1)

@@ -23,7 +23,11 @@ X_TILE = 512
 CHUNKS = [(0, 512), (512, 512), (1024, 512), (1536, 256), (1792, 256)]
 F_TILES = FILTERS // P
 C_TILES = CHANNELS // P
-LAG = 5
+WARM = 20
+K0, RN, RD = 12, 1, 2
+VECTOR_UNITS = ((), 4)
+X_HEAD = 1024
+W_COLS = 128
 
 
 def tile_filter_bank_channel_mixer_s4_kernel(
@@ -53,14 +57,16 @@ def tile_filter_bank_channel_mixer_s4_kernel(
             bs_sb.append(st)
         m_sb = keep.tile([P, PASSES, 4 * CHANNELS], U8, name="mixw", align_bytes=64)
         bs_raw = keep.tile([P, PASSES * FILTERS], U8, name="bsraw", align_bytes=64)
-        xs_first = keep.tile([P, PASSES * X_TILE], U8, name="xsfirst", align_bytes=64)
-        xs_rest = keep.tile([P, PASSES * (FRAMES - X_TILE)], U8, name="xsrest", align_bytes=64)
+        xs_head = keep.tile([P, PASSES * X_HEAD], U8, name="xshead", align_bytes=64)
+        xs_rest = keep.tile([P, PASSES * (FRAMES - X_HEAD)], U8, name="xsrest", align_bytes=64)
         ms = keep.tile([P, PASSES * CHANNELS], U8, name="ms", align_bytes=64)
         gain_bf = keep.tile([P, F_TILES], BF16, name="gainbf")
         gain_f = keep.tile([P, F_TILES], F32, name="gainf")
         sgn = keep.tile([P, F_TILES], F32, name="sgn")
         bias_bf = keep.tile([P, C_TILES, 2], BF16, name="biasbf")
-        bias_f = keep.tile([P, C_TILES], F32, name="biasf")
+        warm = keep.tile([P, 4 * W_COLS], BF16, name="warm", align_bytes=64)
+        warm_c = keep.tile([P, W_COLS], U32, name="warmc", align_bytes=64)
+        warm_s = keep.tile([P, W_COLS], U8, name="warms", align_bytes=64)
         dummy = keep.tile([P, 1], F32, name="dummy")
 
         def load_bank(h):
@@ -75,14 +81,27 @@ def tile_filter_bank_channel_mixer_s4_kernel(
                 in_=x_words[:, :, 2 * X_TILE * j : 2 * X_TILE * (j + 1)].rearrange("g p b -> p g b"),
             )
 
-        def load_scales(tile, src, r):
-            nc.sync.dma_start(
+        def load_scales(eng, tile, src, r):
+            eng.dma_start(
                 out=tile[r:P:32, :].rearrange("p (g n) -> p g n", g=PASSES).bitcast(I32),
                 in_=src.rearrange("g (q r) n -> r q g n", r=4)[r].bitcast(I32),
             )
 
         nc.vector.memset(bs_raw[:].bitcast(I32), 0)
-        nc.vector.memset(xs_first[:].bitcast(I32), 0)
+        nc.vector.memset(xs_head[:].bitcast(I32), 0)
+        nc.vector.memset(warm[:], 1.0)
+        nc.vector.quantize_mx(out=warm_c[:].bitcast(FP8X4), scales=warm_s[:], in_=warm[:])
+        for u in range(WARM):
+            wz = psum.tile([P, W_COLS], F32, name="z", tag="z", bufs=4)
+            nc.tensor.matmul_mx(
+                out=wz[:],
+                lhsT=warm_c[:, 0:P].bitcast(FP8X4),
+                lhsT_scale=warm_s[:, 0:P],
+                rhs=warm_c[:].bitcast(FP8X4),
+                rhs_scale=warm_s[:],
+                start=True,
+                stop=True,
+            )
         nc.vector.memset(xs_rest[:].bitcast(I32), 0)
         nc.vector.memset(ms[:].bitcast(I32), 0)
         nc.vector.memset(dummy[:], 0.0)
@@ -93,19 +112,20 @@ def tile_filter_bank_channel_mixer_s4_kernel(
             out=x_sb[0][:].bitcast(I32),
             in_=x_words[:, :, 0 : 2 * X_TILE].rearrange("g p b -> p g b").bitcast(I32),
         )
+        load_scales(nc.gpsimd, xs_head, x_scales[:, :, 0:X_HEAD], 3)
         nc.gpsimd.dma_start(
             out=gain_bf[:].rearrange("p (h t) -> p h t", t=PACK), in_=gain.rearrange("(h p t) -> p h t", p=P, t=PACK)
         )
         for r in range(4):
-            load_scales(bs_raw, bank_scales, r)
-        for r in range(4):
-            load_scales(xs_first, x_scales[:, :, 0:X_TILE], r)
+            load_scales(nc.sync, bs_raw, bank_scales, r)
+        for r in range(3):
+            load_scales(nc.sync, xs_head, x_scales[:, :, 0:X_HEAD], r)
+        load_x(1)
         load_bank(1)
         for r in range(4):
-            load_scales(xs_rest, x_scales[:, :, X_TILE:FRAMES], r)
-        load_x(1)
+            load_scales(nc.sync, xs_rest, x_scales[:, :, X_HEAD:FRAMES], r)
         for r in range(4):
-            load_scales(ms, mix_scales, r)
+            load_scales(nc.sync, ms, mix_scales, r)
         nc.sync.dma_start(out=m_sb[:], in_=mix_words.rearrange("g p n t -> p g (n t)"))
         nc.gpsimd.dma_start(
             out=bias_bf[:, :, 0:1], in_=bias.rearrange("(c p o) -> p c o", p=P, o=1)
@@ -131,13 +151,12 @@ def tile_filter_bank_channel_mixer_s4_kernel(
         zmap = {}
 
         def x_scale_columns(g, n0, w):
-            if n0 < X_TILE:
-                return xs_first[:, g * X_TILE + n0 : g * X_TILE + n0 + w]
-            start = g * (FRAMES - X_TILE) + n0 - X_TILE
+            if n0 < X_HEAD:
+                return xs_head[:, g * X_HEAD + n0 : g * X_HEAD + n0 + w]
+            start = g * (FRAMES - X_HEAD) + n0 - X_HEAD
             return xs_rest[:, start : start + w]
 
-        def bank_pass(k):
-            i, f = divmod(k, F_TILES)
+        def bank_pass(i, f):
             n0, w = CHUNKS[i]
             j, o = divmod(n0, X_TILE)
             y = psum.tile([P, w], F32, name="y", tag="y", bufs=4)
@@ -151,21 +170,19 @@ def tile_filter_bank_channel_mixer_s4_kernel(
                     start=(g == 0),
                     stop=(g == PASSES - 1),
                 )
-            ymap[k] = y
+            ymap[(i, f)] = y
 
-        def rectify(k):
-            i, f = divmod(k, F_TILES)
+        def rectify(i, f):
             h, t = divmod(f, PACK)
             w = CHUNKS[i][1]
             if t == 0:
-                s = work.tile([P, PACK, w], BF16, name="s", tag="s", bufs=3, align_bytes=64)
+                s = work.tile([P, PACK, w], BF16, name="s", tag="s", bufs=4, align_bytes=64)
                 sub[(i, h)] = s
             nc.scalar.activation(
-                out=sub[(i, h)][:, t, :], in_=ymap[k][:], func=ACT.Abs, scale=gain_f[:, f : f + 1]
+                out=sub[(i, h)][:, t, :], in_=ymap[(i, f)][:], func=ACT.Abs, scale=gain_f[:, f : f + 1]
             )
 
-        def sign(k):
-            i, f = divmod(k, F_TILES)
+        def sign(i, f):
             h, t = divmod(f, PACK)
             nc.vector.tensor_scalar(
                 out=sub[(i, h)][:, t, :], in0=sub[(i, h)][:, t, :], scalar1=sgn[:, f : f + 1], scalar2=None, op0=ALU.mult
@@ -179,8 +196,8 @@ def tile_filter_bank_channel_mixer_s4_kernel(
 
         def quantize(i, h):
             w = CHUNKS[i][1]
-            c = work.tile([P, w], U32, name="hc", tag="hc", bufs=4, align_bytes=64)
-            sc = work.tile([P, w], U8, name="hs", tag="hs", bufs=4, align_bytes=64)
+            c = work.tile([P, w], U32, name="hc", tag="hc", bufs=6, align_bytes=64)
+            sc = work.tile([P, w], U8, name="hs", tag="hs", bufs=6, align_bytes=64)
             nc.vector.quantize_mx(
                 out=c[:].bitcast(FP8X4), scales=sc[:], in_=grouped[(i, h)][:].rearrange("p n t -> p (n t)")
             )
@@ -208,10 +225,10 @@ def tile_filter_bank_channel_mixer_s4_kernel(
             z = zmap[(i, c)]
             if on_vector:
                 nc.vector.tensor_scalar(
-                    out=o[:], in0=z[:], scalar1=bias_f[:, c : c + 1], scalar2=None, op0=ALU.add
+                    out=o[:], in0=z[:], scalar1=bias_bf[:, c, 0:1], scalar2=None, op0=ALU.add
                 )
             else:
-                nc.scalar.activation(out=o[:], in_=z[:], func=ACT.Identity, bias=bias_f[:, c : c + 1])
+                nc.scalar.activation(out=o[:], in_=z[:], func=ACT.Identity, bias=bias_bf[:, c, 0:1])
             nc.sync.dma_start(out=out[P * c : P * (c + 1), n0 : n0 + w], in_=o[:])
 
         for f in range(PACK):
@@ -220,35 +237,43 @@ def tile_filter_bank_channel_mixer_s4_kernel(
         nc.vector.tensor_scalar(out=sgn[:], in0=gain_f[:], scalar1=0.0, scalar2=2.0, op0=ALU.is_ge, op1=ALU.mult)
         nc.vector.tensor_scalar(out=sgn[:], in0=sgn[:], scalar1=-1.0, scalar2=None, op0=ALU.add)
 
-        steps = len(CHUNKS) * F_TILES
-        for k in range(steps + 1):
-            if k < steps:
-                bank_pass(k)
-                rectify(k)
-            if k >= 1:
-                sign(k - 1)
-            if k < PACK:
-                permute(PACK + k)
-            if k == 4:
-                nc.vector.tensor_copy(out=bias_f[:], in_=bias_bf[:, :, 0])
-            d = k - (F_TILES - 1 + LAG)
-            if k < steps and d >= 0 and d % 2 == 0:
-                i, c = divmod(d // 2, C_TILES)
-                for g in range(PASSES):
-                    mix_pass(i, c, g)
-                finish(i, c, c == 1)
-            if k >= 4 and k % 4 == 0:
-                interleave((k - 1) // F_TILES, ((k - 1) // PACK) % 2)
-            if k >= 5 and k % 4 == 1:
-                quantize((k - 2) // F_TILES, ((k - 2) // PACK) % 2)
+        order = [(i, f) for i in range(len(CHUNKS)) for f in range(F_TILES)]
         last = len(CHUNKS) - 1
+        tasks = []
+        emitted = 0
+        for k, (i, f) in enumerate(order):
+            bank_pass(i, f)
+            rectify(i, f)
+            if k >= 1:
+                pi, pf = order[k - 1]
+                sign(pi, pf)
+                if pf % PACK == PACK - 1:
+                    tasks += [(interleave, (pi, pf // PACK)), (quantize, (pi, pf // PACK))]
+            if PACK + k < F_TILES:
+                permute(PACK + k)
+            for u in range(2 if len(tasks) > 2 else 1):
+                if tasks:
+                    what, args = tasks.pop(0)
+                    what(*args)
+            mi, c = divmod(emitted, C_TILES)
+            if (k - K0) * RN >= (emitted + 1) * RD and (mi, 1) in codes:
+                emitted += 1
+                for g in range(PASSES):
+                    mix_pass(mi, c, g)
+                if emitted % VECTOR_UNITS[1] in VECTOR_UNITS[0]:
+                    tasks.append((finish, (mi, c, True)))
+                else:
+                    finish(mi, c, False)
+        sign(last, F_TILES - 1)
+        for what, args in tasks:
+            what(*args)
+        interleave(last, 1)
         quantize(last, 1)
-        first_left = (steps - 1 - (F_TILES - 1 + LAG)) // 2 + 1
-        for u in range(first_left, last * C_TILES):
-            i, c = divmod(u, C_TILES)
+        for u in range(emitted, last * C_TILES):
+            mi, c = divmod(u, C_TILES)
             for g in range(PASSES):
-                mix_pass(i, c, g)
-            finish(i, c, c == 1)
+                mix_pass(mi, c, g)
+            finish(mi, c, False)
         for g in range(PASSES):
             for c in range(C_TILES):
                 mix_pass(last, c, g)

@@ -20,12 +20,12 @@ PACK = 4
 K_PASS = P * PACK
 PASSES = 2
 X_TILE = 512
-CHUNKS = [(0, 512), (512, 512), (1024, 512), (1536, 256), (1792, 256)]
+CHUNKS = [(0, 512), (512, 512), (1024, 512), (1536, 512)]
 F_TILES = FILTERS // P
 C_TILES = CHANNELS // P
-WARM = 20
-K0, RN, RD = 12, 1, 2
-VECTOR_UNITS = ((), 4)
+WARM = 30
+K0, RN, RD = 15, 1, 2
+VECTOR_UNITS = ((2,), 4)
 X_HEAD = 1024
 W_COLS = 128
 
@@ -69,16 +69,16 @@ def tile_filter_bank_channel_mixer_s4_kernel(
         warm_s = keep.tile([P, W_COLS], U8, name="warms", align_bytes=64)
         dummy = keep.tile([P, 1], F32, name="dummy")
 
-        def load_bank(h):
-            nc.sync.dma_start(
-                out=b_raw[h][:],
-                in_=bank_words[:, :, 2 * K_PASS * h : 2 * K_PASS * (h + 1)].rearrange("g p b -> p g b"),
+        def load_bank(eng, h):
+            eng.dma_start(
+                out=b_raw[h][:].bitcast(I32),
+                in_=bank_words[:, :, 2 * K_PASS * h : 2 * K_PASS * (h + 1)].rearrange("g p b -> p g b").bitcast(I32),
             )
 
-        def load_x(j):
-            nc.sync.dma_start(
-                out=x_sb[j][:],
-                in_=x_words[:, :, 2 * X_TILE * j : 2 * X_TILE * (j + 1)].rearrange("g p b -> p g b"),
+        def load_x(eng, j):
+            eng.dma_start(
+                out=x_sb[j][:].bitcast(I32),
+                in_=x_words[:, :, 2 * X_TILE * j : 2 * X_TILE * (j + 1)].rearrange("g p b -> p g b").bitcast(I32),
             )
 
         def load_scales(eng, tile, src, r):
@@ -107,12 +107,7 @@ def tile_filter_bank_channel_mixer_s4_kernel(
         nc.vector.memset(dummy[:], 0.0)
         nc.scalar.activation(out=dummy[:], in_=dummy[:], func=ACT.Abs)
 
-        load_bank(0)
-        nc.gpsimd.dma_start(
-            out=x_sb[0][:].bitcast(I32),
-            in_=x_words[:, :, 0 : 2 * X_TILE].rearrange("g p b -> p g b").bitcast(I32),
-        )
-        load_scales(nc.gpsimd, xs_head, x_scales[:, :, 0:X_HEAD], 3)
+        load_x(nc.gpsimd, 0)
         nc.gpsimd.dma_start(
             out=gain_bf[:].rearrange("p (h t) -> p h t", t=PACK), in_=gain.rearrange("(h p t) -> p h t", p=P, t=PACK)
         )
@@ -120,25 +115,30 @@ def tile_filter_bank_channel_mixer_s4_kernel(
             load_scales(nc.sync, bs_raw, bank_scales, r)
         for r in range(3):
             load_scales(nc.sync, xs_head, x_scales[:, :, 0:X_HEAD], r)
-        load_x(1)
-        load_bank(1)
+        load_bank(nc.sync, 0)
+        load_scales(nc.sync, xs_head, x_scales[:, :, 0:X_HEAD], 3)
+        load_bank(nc.sync, 1)
+        load_x(nc.sync, 1)
         for r in range(4):
             load_scales(nc.sync, xs_rest, x_scales[:, :, X_HEAD:FRAMES], r)
         for r in range(4):
             load_scales(nc.sync, ms, mix_scales, r)
         nc.sync.dma_start(out=m_sb[:], in_=mix_words.rearrange("g p n t -> p g (n t)"))
-        nc.gpsimd.dma_start(
+        nc.sync.dma_start(
             out=bias_bf[:, :, 0:1], in_=bias.rearrange("(c p o) -> p c o", p=P, o=1)
         )
-        load_x(2)
-        load_x(3)
+        load_x(nc.sync, 2)
+        load_x(nc.sync, 3)
 
-        def permute(f):
+        def permute_codes(f):
             h, t = divmod(f, PACK)
             nc.vector.tensor_copy(
                 out=b_sb[f][:].rearrange("p g (m b) -> p g m b", b=2),
                 in_=b_raw[h][:].rearrange("p g (m t b) -> p t g m b", t=PACK, b=2)[:, t],
             )
+
+        def permute_scales(f):
+            h, t = divmod(f, PACK)
             nc.vector.tensor_copy(
                 out=bs_sb[f][:],
                 in_=bs_raw[:].rearrange("p (g h m t) -> p h t g m", g=PASSES, h=2, t=PACK)[:, h, t],
@@ -191,7 +191,9 @@ def tile_filter_bank_channel_mixer_s4_kernel(
         def interleave(i, h):
             w = CHUNKS[i][1]
             gr = work.tile([P, w, PACK], BF16, name="gr", tag="gr", bufs=3, align_bytes=64)
-            nc.vector.tensor_copy(out=gr[:], in_=sub[(i, h)][:].rearrange("p t n -> p n t"))
+            nc.vector.tensor_copy(
+                out=gr[:].rearrange("p (c i) t -> p c t i", i=4), in_=sub[(i, h)][:].rearrange("p t (c i) -> p c t i", i=4)
+            )
             grouped[(i, h)] = gr
 
         def quantize(i, h):
@@ -232,7 +234,8 @@ def tile_filter_bank_channel_mixer_s4_kernel(
             nc.sync.dma_start(out=out[P * c : P * (c + 1), n0 : n0 + w], in_=o[:])
 
         for f in range(PACK):
-            permute(f)
+            permute_codes(f)
+            permute_scales(f)
         nc.vector.tensor_copy(out=gain_f[:], in_=gain_bf[:])
         nc.vector.tensor_scalar(out=sgn[:], in0=gain_f[:], scalar1=0.0, scalar2=2.0, op0=ALU.is_ge, op1=ALU.mult)
         nc.vector.tensor_scalar(out=sgn[:], in0=sgn[:], scalar1=-1.0, scalar2=None, op0=ALU.add)
@@ -250,7 +253,8 @@ def tile_filter_bank_channel_mixer_s4_kernel(
                 if pf % PACK == PACK - 1:
                     tasks += [(interleave, (pi, pf // PACK)), (quantize, (pi, pf // PACK))]
             if PACK + k < F_TILES:
-                permute(PACK + k)
+                permute_codes(PACK + k)
+                permute_scales(PACK + k)
             for u in range(2 if len(tasks) > 2 else 1):
                 if tasks:
                     what, args = tasks.pop(0)
@@ -267,15 +271,68 @@ def tile_filter_bank_channel_mixer_s4_kernel(
         sign(last, F_TILES - 1)
         for what, args in tasks:
             what(*args)
-        interleave(last, 1)
-        quantize(last, 1)
+        half = CHUNKS[last][1] // 2
+        parts = []
+        for e in range(2):
+            gr = work.tile([P, half, PACK], BF16, name="gr", tag="gr", bufs=3, align_bytes=64)
+            nc.vector.tensor_copy(
+                out=gr[:].rearrange("p (c i) t -> p c t i", i=4),
+                in_=sub[(last, 1)][:, :, half * e : half * (e + 1)].rearrange("p t (c i) -> p c t i", i=4),
+            )
+            parts.append(gr)
+        tails = []
+        for e in range(2):
+            hc = work.tile([P, half], U32, name="hc", tag="hc", bufs=6, align_bytes=64)
+            hs = work.tile([P, half], U8, name="hs", tag="hs", bufs=6, align_bytes=64)
+            nc.vector.quantize_mx(
+                out=hc[:].bitcast(FP8X4), scales=hs[:], in_=parts[e][:].rearrange("p n t -> p (n t)")
+            )
+            tails.append((hc[:], hs[:]))
         for u in range(emitted, last * C_TILES):
             mi, c = divmod(u, C_TILES)
             for g in range(PASSES):
                 mix_pass(mi, c, g)
             finish(mi, c, False)
+        c0, s0 = codes[(last, 0)]
+        ends = {}
         for g in range(PASSES):
-            for c in range(C_TILES):
-                mix_pass(last, c, g)
+            for e in range(2):
+                if g == 0:
+                    hc, hs = c0[:, half * e : half * (e + 1)], s0[:, half * e : half * (e + 1)]
+                else:
+                    hc, hs = tails[e]
+                for c in range(C_TILES):
+                    if g == 0:
+                        if e == 0:
+                            z = psum.tile([P, half], F32, name="z", tag="z", bufs=4)
+                        else:
+                            z = psum.tile([P, half], F32, name="y", tag="y", bufs=4)
+                        ends[(e, c)] = z
+                    nc.tensor.matmul_mx(
+                        out=ends[(e, c)][:],
+                        lhsT=m_sb[:, g, 4 * P * c : 4 * P * (c + 1)].bitcast(FP8X4),
+                        lhsT_scale=ms[:, g * CHANNELS + P * c : g * CHANNELS + P * (c + 1)],
+                        rhs=hc.bitcast(FP8X4),
+                        rhs_scale=hs,
+                        start=(g == 0),
+                        stop=(g == PASSES - 1),
+                    )
+        n0 = CHUNKS[last][0]
+        outs = []
         for c in range(C_TILES):
-            finish(last, c, c % 2 == 1)
+            o = work.tile([P, 2 * half], F32, name="o", tag="o", bufs=6, align_bytes=64)
+            outs.append(o)
+        for e in range(2):
+            for c in range(C_TILES):
+                cols = slice(half * e, half * (e + 1))
+                if c % 2 == 1:
+                    nc.vector.tensor_scalar(
+                        out=outs[c][:, cols], in0=ends[(e, c)][:], scalar1=bias_bf[:, c, 0:1], scalar2=None, op0=ALU.add
+                    )
+                else:
+                    nc.scalar.activation(
+                        out=outs[c][:, cols], in_=ends[(e, c)][:], func=ACT.Identity, bias=bias_bf[:, c, 0:1]
+                    )
+                nc.sync.dma_start(
+                    out=out[P * c : P * (c + 1), n0 + half * e : n0 + half * (e + 1)], in_=outs[c][:, cols]
+                )

@@ -23,9 +23,9 @@ X_TILE = 512
 CHUNKS = [(0, 512), (512, 512), (1024, 512), (1536, 512)]
 F_TILES = FILTERS // P
 C_TILES = CHANNELS // P
-WARM = 30
-K0, RN, RD = 15, 1, 2
-VECTOR_UNITS = ((2,), 4)
+WARM = 40
+K0, RN, RD = 14, 1, 2
+VECTOR_UNITS = ((3,), 4)
 X_HEAD = 1024
 W_COLS = 128
 
@@ -107,22 +107,23 @@ def tile_filter_bank_channel_mixer_s4_kernel(
         nc.vector.memset(dummy[:], 0.0)
         nc.scalar.activation(out=dummy[:], in_=dummy[:], func=ACT.Abs)
 
-        load_x(nc.gpsimd, 0)
-        nc.gpsimd.dma_start(
+        nc.sync.dma_start(
             out=gain_bf[:].rearrange("p (h t) -> p h t", t=PACK), in_=gain.rearrange("(h p t) -> p h t", p=P, t=PACK)
         )
+        load_bank(nc.sync, 0)
         for r in range(4):
             load_scales(nc.sync, bs_raw, bank_scales, r)
-        for r in range(3):
+        for r in range(2):
             load_scales(nc.sync, xs_head, x_scales[:, :, 0:X_HEAD], r)
-        load_bank(nc.sync, 0)
-        load_scales(nc.sync, xs_head, x_scales[:, :, 0:X_HEAD], 3)
+        load_x(nc.sync, 0)
+        for r in range(2, 4):
+            load_scales(nc.sync, xs_head, x_scales[:, :, 0:X_HEAD], r)
         load_bank(nc.sync, 1)
         load_x(nc.sync, 1)
         for r in range(4):
-            load_scales(nc.sync, xs_rest, x_scales[:, :, X_HEAD:FRAMES], r)
-        for r in range(4):
             load_scales(nc.sync, ms, mix_scales, r)
+        for r in range(4):
+            load_scales(nc.sync, xs_rest, x_scales[:, :, X_HEAD:FRAMES], r)
         nc.sync.dma_start(out=m_sb[:], in_=mix_words.rearrange("g p n t -> p g (n t)"))
         nc.sync.dma_start(
             out=bias_bf[:, :, 0:1], in_=bias.rearrange("(c p o) -> p c o", p=P, o=1)
@@ -243,15 +244,18 @@ def tile_filter_bank_channel_mixer_s4_kernel(
         order = [(i, f) for i in range(len(CHUNKS)) for f in range(F_TILES)]
         last = len(CHUNKS) - 1
         tasks = []
+        fresh = []
         emitted = 0
         for k, (i, f) in enumerate(order):
             bank_pass(i, f)
             rectify(i, f)
+            tasks += fresh
+            fresh = []
             if k >= 1:
                 pi, pf = order[k - 1]
                 sign(pi, pf)
                 if pf % PACK == PACK - 1:
-                    tasks += [(interleave, (pi, pf // PACK)), (quantize, (pi, pf // PACK))]
+                    fresh = [(interleave, (pi, pf // PACK)), (quantize, (pi, pf // PACK))]
             if PACK + k < F_TILES:
                 permute_codes(PACK + k)
                 permute_scales(PACK + k)

@@ -23,7 +23,7 @@ X_TILE = 512
 CHUNKS = [(0, 512), (512, 512), (1024, 512), (1536, 512)]
 F_TILES = FILTERS // P
 C_TILES = CHANNELS // P
-WARM = 40
+WARM = 36
 K0, RN, RD = 14, 1, 2
 VECTOR_UNITS = ((3,), 4)
 X_HEAD = 1024
@@ -87,9 +87,9 @@ def tile_filter_bank_channel_mixer_s4_kernel(
                 in_=src.rearrange("g (q r) n -> r q g n", r=4)[r].bitcast(I32),
             )
 
-        nc.vector.memset(bs_raw[:].bitcast(I32), 0)
+        nc.gpsimd.memset(bs_raw[:].bitcast(I32), 0)
         nc.vector.memset(xs_head[:].bitcast(I32), 0)
-        nc.vector.memset(warm[:], 1.0)
+        nc.gpsimd.memset(warm[:].bitcast(U32), 0x3F803F80)
         nc.vector.quantize_mx(out=warm_c[:].bitcast(FP8X4), scales=warm_s[:], in_=warm[:])
         for u in range(WARM):
             wz = psum.tile([P, W_COLS], F32, name="z", tag="z", bufs=4)
@@ -110,13 +110,13 @@ def tile_filter_bank_channel_mixer_s4_kernel(
         nc.sync.dma_start(
             out=gain_bf[:].rearrange("p (h t) -> p h t", t=PACK), in_=gain.rearrange("(h p t) -> p h t", p=P, t=PACK)
         )
-        load_bank(nc.sync, 0)
         for r in range(4):
             load_scales(nc.sync, bs_raw, bank_scales, r)
-        for r in range(2):
+        load_bank(nc.sync, 0)
+        for r in range(1):
             load_scales(nc.sync, xs_head, x_scales[:, :, 0:X_HEAD], r)
         load_x(nc.sync, 0)
-        for r in range(2, 4):
+        for r in range(1, 4):
             load_scales(nc.sync, xs_head, x_scales[:, :, 0:X_HEAD], r)
         load_bank(nc.sync, 1)
         load_x(nc.sync, 1)

from contextlib import ExitStack

import concourse.mybir as mybir

SAMPLES, FRAMES, FILTERS, CHANNELS = 1024, 2048, 1024, 512
FLOPS = 2 * SAMPLES * FRAMES * FILTERS + 2 * FILTERS * FRAMES * CHANNELS

F32 = mybir.dt.float32
BF16 = mybir.dt.bfloat16
I32 = mybir.dt.int32
U32 = mybir.dt.uint32
U8 = mybir.dt.uint8
FP8X4 = mybir.dt.float8_e4m3fn_x4
FP4X4 = mybir.dt.float4_e2m1fn_x4
ALU = mybir.AluOpType
ACT = mybir.ActivationFunctionType

P = 128
PACK = 4
K_PASS = P * PACK
PASSES = 2
X_TILE = 512
CHUNKS = [(0, 512), (512, 512), (1024, 512), (1536, 512)]
F_TILES = FILTERS // P
C_TILES = CHANNELS // P
WARM = 36
K0, RN, RD = 14, 1, 2
VECTOR_UNITS = ((3,), 4)
X_HEAD = 1024
W_COLS = 128


def tile_filter_bank_channel_mixer_s4_kernel(
    tc, x_words, x_scales, bank_words, bank_scales, gain, mix_words, mix_scales, bias, out
):
    nc = tc.nc
    with ExitStack() as ctx:
        keep = ctx.enter_context(tc.tile_pool(name="keep", bufs=1))
        work = ctx.enter_context(tc.tile_pool(name="work", bufs=3))
        psum = ctx.enter_context(tc.psum_pool(name="psum", bufs=4))
        ctx.enter_context(nc.allow_non_contiguous_dma(reason="small gain and bias columns"))
        ctx.enter_context(tc.manual_schedule())

        x_sb = []
        for j in range(FRAMES // X_TILE):
            xt = keep.tile([P, PASSES, 2 * X_TILE], U8, name="x%d" % j, align_bytes=64)
            x_sb.append(xt)
        b_raw = []
        for h in range(2):
            bt = keep.tile([P, PASSES, 2 * K_PASS], U8, name="braw%d" % h, align_bytes=64)
            b_raw.append(bt)
        b_sb, bs_sb = [], []
        for f in range(F_TILES):
            bt = keep.tile([P, PASSES, 2 * P], U8, name="b%d" % f, align_bytes=64)
            b_sb.append(bt)
            st = keep.tile([P, PASSES, P], U8, name="bs%d" % f, align_bytes=64)
            bs_sb.append(st)
        m_sb = keep.tile([P, PASSES, 4 * CHANNELS], U8, name="mixw", align_bytes=64)
        bs_raw = keep.tile([P, PASSES * FILTERS], U8, name="bsraw", align_bytes=64)
        xs_head = keep.tile([P, PASSES * X_HEAD], U8, name="xshead", align_bytes=64)
        xs_rest = keep.tile([P, PASSES * (FRAMES - X_HEAD)], U8, name="xsrest", align_bytes=64)
        ms = keep.tile([P, PASSES * CHANNELS], U8, name="ms", align_bytes=64)
        gain_bf = keep.tile([P, F_TILES], BF16, name="gainbf")
        gain_f = keep.tile([P, F_TILES], F32, name="gainf")
        sgn = keep.tile([P, F_TILES], F32, name="sgn")
        bias_bf = keep.tile([P, C_TILES, 2], BF16, name="biasbf")
        warm = keep.tile([P, 4 * W_COLS], BF16, name="warm", align_bytes=64)
        warm_c = keep.tile([P, W_COLS], U32, name="warmc", align_bytes=64)
        warm_s = keep.tile([P, W_COLS], U8, name="warms", align_bytes=64)
        dummy = keep.tile([P, 1], F32, name="dummy")

        def load_bank(eng, h):
            eng.dma_start(
                out=b_raw[h][:].bitcast(I32),
                in_=bank_words[:, :, 2 * K_PASS * h : 2 * K_PASS * (h + 1)].rearrange("g p b -> p g b").bitcast(I32),
            )

        def load_x(eng, j):
            eng.dma_start(
                out=x_sb[j][:].bitcast(I32),
                in_=x_words[:, :, 2 * X_TILE * j : 2 * X_TILE * (j + 1)].rearrange("g p b -> p g b").bitcast(I32),
            )

        def load_scales(eng, tile, src, r):
            eng.dma_start(
                out=tile[r:P:32, :].rearrange("p (g n) -> p g n", g=PASSES).bitcast(I32),
                in_=src.rearrange("g (q r) n -> r q g n", r=4)[r].bitcast(I32),
            )

        nc.gpsimd.memset(bs_raw[:].bitcast(I32), 0)
        nc.vector.memset(xs_head[:].bitcast(I32), 0)
        nc.gpsimd.memset(warm[:].bitcast(U32), 0x3F803F80)
        nc.vector.quantize_mx(out=warm_c[:].bitcast(FP8X4), scales=warm_s[:], in_=warm[:])
        for u in range(WARM):
            wz = psum.tile([P, W_COLS], F32, name="z", tag="z", bufs=4)
            nc.tensor.matmul_mx(
                out=wz[:],
                lhsT=warm_c[:, 0:P].bitcast(FP8X4),
                lhsT_scale=warm_s[:, 0:P],
                rhs=warm_c[:].bitcast(FP8X4),
                rhs_scale=warm_s[:],
                start=True,
                stop=True,
            )
        nc.vector.memset(xs_rest[:].bitcast(I32), 0)
        nc.vector.memset(ms[:].bitcast(I32), 0)
        nc.vector.memset(dummy[:], 0.0)
        nc.scalar.activation(out=dummy[:], in_=dummy[:], func=ACT.Abs)

        nc.sync.dma_start(
            out=gain_bf[:].rearrange("p (h t) -> p h t", t=PACK), in_=gain.rearrange("(h p t) -> p h t", p=P, t=PACK)
        )
        for r in range(4):
            load_scales(nc.sync, bs_raw, bank_scales, r)
        load_bank(nc.sync, 0)
        for r in range(1):
            load_scales(nc.sync, xs_head, x_scales[:, :, 0:X_HEAD], r)
        load_x(nc.sync, 0)
        for r in range(1, 4):
            load_scales(nc.sync, xs_head, x_scales[:, :, 0:X_HEAD], r)
        load_bank(nc.sync, 1)
        load_x(nc.sync, 1)
        for r in range(4):
            load_scales(nc.sync, ms, mix_scales, r)
        for r in range(4):
            load_scales(nc.sync, xs_rest, x_scales[:, :, X_HEAD:FRAMES], r)
        nc.sync.dma_start(out=m_sb[:], in_=mix_words.rearrange("g p n t -> p g (n t)"))
        nc.sync.dma_start(
            out=bias_bf[:, :, 0:1], in_=bias.rearrange("(c p o) -> p c o", p=P, o=1)
        )
        load_x(nc.sync, 2)
        load_x(nc.sync, 3)

        def permute_codes(f):
            h, t = divmod(f, PACK)
            nc.vector.tensor_copy(
                out=b_sb[f][:].rearrange("p g (m b) -> p g m b", b=2),
                in_=b_raw[h][:].rearrange("p g (m t b) -> p t g m b", t=PACK, b=2)[:, t],
            )

        def permute_scales(f):
            h, t = divmod(f, PACK)
            nc.vector.tensor_copy(
                out=bs_sb[f][:],
                in_=bs_raw[:].rearrange("p (g h m t) -> p h t g m", g=PASSES, h=2, t=PACK)[:, h, t],
            )

        sub = {}
        ymap = {}
        grouped = {}
        codes = {}
        zmap = {}

        def x_scale_columns(g, n0, w):
            if n0 < X_HEAD:
                return xs_head[:, g * X_HEAD + n0 : g * X_HEAD + n0 + w]
            start = g * (FRAMES - X_HEAD) + n0 - X_HEAD
            return xs_rest[:, start : start + w]

        def bank_pass(i, f):
            n0, w = CHUNKS[i]
            j, o = divmod(n0, X_TILE)
            y = psum.tile([P, w], F32, name="y", tag="y", bufs=4)
            for g in range(PASSES):
                nc.tensor.matmul_mx(
                    out=y[:],
                    lhsT=b_sb[f][:, g, :].bitcast(FP4X4),
                    lhsT_scale=bs_sb[f][:, g, :],
                    rhs=x_sb[j][:, g, 2 * o : 2 * (o + w)].bitcast(FP4X4),
                    rhs_scale=x_scale_columns(g, n0, w),
                    start=(g == 0),
                    stop=(g == PASSES - 1),
                )
            ymap[(i, f)] = y

        def rectify(i, f):
            h, t = divmod(f, PACK)
            w = CHUNKS[i][1]
            if t == 0:
                s = work.tile([P, PACK, w], BF16, name="s", tag="s", bufs=4, align_bytes=64)
                sub[(i, h)] = s
            nc.scalar.activation(
                out=sub[(i, h)][:, t, :], in_=ymap[(i, f)][:], func=ACT.Abs, scale=gain_f[:, f : f + 1]
            )

        def sign(i, f):
            h, t = divmod(f, PACK)
            nc.vector.tensor_scalar(
                out=sub[(i, h)][:, t, :], in0=sub[(i, h)][:, t, :], scalar1=sgn[:, f : f + 1], scalar2=None, op0=ALU.mult
            )

        def interleave(i, h):
            w = CHUNKS[i][1]
            gr = work.tile([P, w, PACK], BF16, name="gr", tag="gr", bufs=3, align_bytes=64)
            nc.vector.tensor_copy(
                out=gr[:].rearrange("p (c i) t -> p c t i", i=4), in_=sub[(i, h)][:].rearrange("p t (c i) -> p c t i", i=4)
            )
            grouped[(i, h)] = gr

        def quantize(i, h):
            w = CHUNKS[i][1]
            c = work.tile([P, w], U32, name="hc", tag="hc", bufs=6, align_bytes=64)
            sc = work.tile([P, w], U8, name="hs", tag="hs", bufs=6, align_bytes=64)
            nc.vector.quantize_mx(
                out=c[:].bitcast(FP8X4), scales=sc[:], in_=grouped[(i, h)][:].rearrange("p n t -> p (n t)")
            )
            codes[(i, h)] = (c, sc)

        def mix_pass(i, c, g):
            w = CHUNKS[i][1]
            if g == 0:
                z = psum.tile([P, w], F32, name="z", tag="z", bufs=4)
                zmap[(i, c)] = z
            hc, hs = codes[(i, g)]
            nc.tensor.matmul_mx(
                out=zmap[(i, c)][:],
                lhsT=m_sb[:, g, 4 * P * c : 4 * P * (c + 1)].bitcast(FP8X4),
                lhsT_scale=ms[:, g * CHANNELS + P * c : g * CHANNELS + P * (c + 1)],
                rhs=hc[:].bitcast(FP8X4),
                rhs_scale=hs[:],
                start=(g == 0),
                stop=(g == PASSES - 1),
            )

        def finish(i, c, on_vector):
            n0, w = CHUNKS[i]
            o = work.tile([P, w], F32, name="o", tag="o", bufs=6, align_bytes=64)
            z = zmap[(i, c)]
            if on_vector:
                nc.vector.tensor_scalar(
                    out=o[:], in0=z[:], scalar1=bias_bf[:, c, 0:1], scalar2=None, op0=ALU.add
                )
            else:
                nc.scalar.activation(out=o[:], in_=z[:], func=ACT.Identity, bias=bias_bf[:, c, 0:1])
            nc.sync.dma_start(out=out[P * c : P * (c + 1), n0 : n0 + w], in_=o[:])

        for f in range(PACK):
            permute_codes(f)
            permute_scales(f)
        nc.vector.tensor_copy(out=gain_f[:], in_=gain_bf[:])
        nc.vector.tensor_scalar(out=sgn[:], in0=gain_f[:], scalar1=0.0, scalar2=2.0, op0=ALU.is_ge, op1=ALU.mult)
        nc.vector.tensor_scalar(out=sgn[:], in0=sgn[:], scalar1=-1.0, scalar2=None, op0=ALU.add)

        order = [(i, f) for i in range(len(CHUNKS)) for f in range(F_TILES)]
        last = len(CHUNKS) - 1
        tasks = []
        fresh = []
        emitted = 0
        for k, (i, f) in enumerate(order):
            bank_pass(i, f)
            rectify(i, f)
            tasks += fresh
            fresh = []
            if k >= 1:
                pi, pf = order[k - 1]
                sign(pi, pf)
                if pf % PACK == PACK - 1:
                    fresh = [(interleave, (pi, pf // PACK)), (quantize, (pi, pf // PACK))]
            if PACK + k < F_TILES:
                permute_codes(PACK + k)
                permute_scales(PACK + k)
            for u in range(2 if len(tasks) > 2 else 1):
                if tasks:
                    what, args = tasks.pop(0)
                    what(*args)
            mi, c = divmod(emitted, C_TILES)
            if (k - K0) * RN >= (emitted + 1) * RD and (mi, 1) in codes:
                emitted += 1
                for g in range(PASSES):
                    mix_pass(mi, c, g)
                if emitted % VECTOR_UNITS[1] in VECTOR_UNITS[0]:
                    tasks.append((finish, (mi, c, True)))
                else:
                    finish(mi, c, False)
        sign(last, F_TILES - 1)
        for what, args in tasks:
            what(*args)
        half = CHUNKS[last][1] // 2
        parts = []
        for e in range(2):
            gr = work.tile([P, half, PACK], BF16, name="gr", tag="gr", bufs=3, align_bytes=64)
            nc.vector.tensor_copy(
                out=gr[:].rearrange("p (c i) t -> p c t i", i=4),
                in_=sub[(last, 1)][:, :, half * e : half * (e + 1)].rearrange("p t (c i) -> p c t i", i=4),
            )
            parts.append(gr)
        tails = []
        for e in range(2):
            hc = work.tile([P, half], U32, name="hc", tag="hc", bufs=6, align_bytes=64)
            hs = work.tile([P, half], U8, name="hs", tag="hs", bufs=6, align_bytes=64)
            nc.vector.quantize_mx(
                out=hc[:].bitcast(FP8X4), scales=hs[:], in_=parts[e][:].rearrange("p n t -> p (n t)")
            )
            tails.append((hc[:], hs[:]))
        for u in range(emitted, last * C_TILES):
            mi, c = divmod(u, C_TILES)
            for g in range(PASSES):
                mix_pass(mi, c, g)
            finish(mi, c, False)
        c0, s0 = codes[(last, 0)]
        ends = {}
        for g in range(PASSES):
            for e in range(2):
                if g == 0:
                    hc, hs = c0[:, half * e : half * (e + 1)], s0[:, half * e : half * (e + 1)]
                else:
                    hc, hs = tails[e]
                for c in range(C_TILES):
                    if g == 0:
                        if e == 0:
                            z = psum.tile([P, half], F32, name="z", tag="z", bufs=4)
                        else:
                            z = psum.tile([P, half], F32, name="y", tag="y", bufs=4)
                        ends[(e, c)] = z
                    nc.tensor.matmul_mx(
                        out=ends[(e, c)][:],
                        lhsT=m_sb[:, g, 4 * P * c : 4 * P * (c + 1)].bitcast(FP8X4),
                        lhsT_scale=ms[:, g * CHANNELS + P * c : g * CHANNELS + P * (c + 1)],
                        rhs=hc.bitcast(FP8X4),
                        rhs_scale=hs,
                        start=(g == 0),
                        stop=(g == PASSES - 1),
                    )
        n0 = CHUNKS[last][0]
        outs = []
        for c in range(C_TILES):
            o = work.tile([P, 2 * half], F32, name="o", tag="o", bufs=6, align_bytes=64)
            outs.append(o)
        for e in range(2):
            for c in range(C_TILES):
                cols = slice(half * e, half * (e + 1))
                if c % 2 == 1:
                    nc.vector.tensor_scalar(
                        out=outs[c][:, cols], in0=ends[(e, c)][:], scalar1=bias_bf[:, c, 0:1], scalar2=None, op0=ALU.add
                    )
                else:
                    nc.scalar.activation(
                        out=outs[c][:, cols], in_=ends[(e, c)][:], func=ACT.Identity, bias=bias_bf[:, c, 0:1]
                    )
                nc.sync.dma_start(
                    out=out[P * c : P * (c + 1), n0 + half * e : n0 + half * (e + 1)], in_=outs[c][:, cols]
                )
